import numpy as np
import ml_dtypes


def mxq(x, axis, fmt="e4m3"):
    dtype, down = {"e4m3": (ml_dtypes.float8_e4m3fn, 7), "e5m2": (ml_dtypes.float8_e5m2, 14)}[fmt]
    v = np.moveaxis(np.asarray(x, np.float32).astype(ml_dtypes.bfloat16).astype(np.float64), axis, -1)
    blocks = v.reshape(v.shape[:-1] + (-1, 32))
    amax = np.abs(blocks).max(-1, keepdims=True)
    byte = np.maximum(np.where(amax > 0, np.frexp(amax)[1] - 1 + 127, 0) - down, 1)
    scale = np.exp2(byte - 127.0)
    codes = (blocks / scale).astype(np.float32).astype(dtype).astype(np.float64)
    return np.moveaxis((codes * scale).reshape(v.shape), -1, axis)


WIDE = False


def mx_kscale(k):
    if not WIDE:
        return np.ones(k)
    levels = np.array([10, -10, 5, -5, 0])
    if k % 512:
        return np.exp2(np.random.permutation(np.resize(levels, k // 32))).repeat(32)
    a = np.empty((k // 512, 16))
    for p in range(k // 512):
        a[p, :8] = np.random.permutation(np.resize(levels, 8))
        for g in range(8):
            far = levels[np.abs(levels - a[p, g]) >= 10]
            a[p, g + 8] = far[np.random.randint(len(far))]
    return np.exp2(a.ravel()).repeat(32)


def f64(x):
    return np.asarray(x).astype(np.float64)


def striped(idx):
    return np.tile(idx.reshape(-1, 16).T, (8, 1)).astype(np.uint16)


def unstriped(offs):
    return offs[:16].T.reshape(-1).astype(np.int64)


def striped8(idx):
    return np.concatenate([x.reshape(-1, 16).T for x in idx]).astype(np.uint16)


def runs(offs, k):
    lists = np.stack([offs[16 * r : 16 * r + 16].T.reshape(-1) for r in range(8)]).astype(np.int64)
    return lists[np.arange(k) % 512 // 64]


def pack_weight(w):
    k, n = w.shape
    w = f64(np.asarray(w, np.float32).astype(ml_dtypes.bfloat16)).reshape(k // 32, 32, n)
    amax = np.abs(w).max(1)
    byte = np.clip(np.where(amax > 0, np.frexp(amax)[1] - 1 + 127 - 7, 1), 1, 254)
    scaled = (w * np.exp2(127.0 - byte)[:, None, :]).reshape(k, n).astype(np.float32)
    words = np.ascontiguousarray(scaled.reshape(k // 512, 128, 4, n).transpose(0, 1, 3, 2)).astype(ml_dtypes.float8_e4m3fn).view(np.uint8)
    return words, np.ascontiguousarray(byte.astype(np.uint8).reshape(k // 512, 16, n))


def unpack_weight(words, scales):
    g, p, n, _ = words.shape
    vals = np.ascontiguousarray(words).view(ml_dtypes.float8_e4m3fn).astype(np.float64) * np.repeat(np.exp2(scales.astype(np.float64) - 127.0), 8, axis=1)[..., None]
    return vals.transpose(0, 1, 3, 2).reshape(g * 512, n)


def relu(v):
    return np.maximum(v, 0.0)

def planes(y):
    n, m = y.shape
    v = y.astype(np.float32).astype(ml_dtypes.bfloat16).astype(np.float64).reshape(n // 32, 32, m)
    top = np.abs(v).max(1)
    byte = np.clip(np.where(top > 0, np.frexp(top)[1] - 1 + 127 - 7, 1), 1, 254)
    codes = (v * np.exp2(127.0 - byte)[:, None, :]).reshape(n, m).astype(np.float32).astype(ml_dtypes.float8_e4m3fn).view(np.uint8)
    words = codes.reshape(n // 512, 128, 4, m).transpose(0, 1, 3, 2)
    return np.ascontiguousarray(words), np.ascontiguousarray(byte.astype(np.uint8).reshape(n // 512, 16, m))


K, T, S, N, G, H = 512, 1024, 256, 512, 2048, 512


def setup_inputs():
    n = np.random.standard_normal
    s = mx_kscale(K)[:, None]
    u = mx_kscale(K)
    packed_xT = pack_weight(n((K, T)) * s)
    packed_dT = pack_weight(n((K, G)) / s)
    packed_w1 = pack_weight(n((H, N)) / np.sqrt(2 * H) / u[:, None])
    packed_w2 = pack_weight(n((K, N)) / np.sqrt(2 * K) / s)
    return {
        "x_words": packed_xT[0],
        "x_scales": packed_xT[1],
        "d_words": packed_dT[0],
        "d_scales": packed_dT[1],
        "gn": (np.random.uniform(0.5, 1.5, (H, 1)) * u[:, None]).astype(np.float32),
        "w1_words": packed_w1[0],
        "w1_scales": packed_w1[1],
        "w2_words": packed_w2[0],
        "w2_scales": packed_w2[1],
        "offs": striped(np.random.permutation(T)[:S]),
        "k1": striped8(np.random.randint(0, G, (8, H))),
        "n1": striped(np.random.permutation(S)),
        "n2": striped(np.random.permutation(S)),
        "two": striped(np.random.permutation(T)[:S]),
        "n3": striped(np.random.permutation(S)),
    }


def reference(x_words, x_scales, d_words, d_scales, gn, w1_words, w1_scales, w2_words, w2_scales, offs, k1, n1, n2, two, n3):
    d_k1 = unpack_weight(d_words, d_scales)[np.arange(K)[:, None], runs(k1, K)]
    xq = unpack_weight(x_words, x_scales)[:, unstriped(offs)]
    h = 0.0625 * (d_k1.T @ xq)
    st = h + h[:, unstriped(n1)]
    z = f64(gn) * (st * (np.tanh(st[:, unstriped(n2)])))
    x_two = unpack_weight(x_words, x_scales)[:, unstriped(two)]
    h2 = unpack_weight(w1_words, w1_scales).T @ mxq(z, 0, "e4m3") + unpack_weight(w2_words, w2_scales).T @ x_two
    rl = relu(h2)
    ds = np.zeros((N, S))
    ds[:, unstriped(n3)] = rl
    out_0 = ds - (0.5 * h2)
    return (out_0,) + planes(out_0)

@@ -1,0 +1,183 @@
+from contextlib import ExitStack
+
+import concourse.mybir as mybir
+
+K, T, S, N, G, H = 512, 1024, 256, 512, 2048, 512
+FLOPS = 2 * K * H * S + 2 * H * N * S + 2 * K * N * S
+
+F32 = mybir.dt.float32
+BF16 = mybir.dt.bfloat16
+I32 = mybir.dt.int32
+U32 = mybir.dt.uint32
+U16 = mybir.dt.uint16
+U8 = mybir.dt.uint8
+FP8X4 = mybir.dt.float8_e4m3fn_x4
+ALU = mybir.AluOpType
+ACT = mybir.ActivationFunctionType
+
+P = 128
+PACK = 4
+HALF = S // 2
+SPARE = 16
+
+
+def words_in_dram(words):
+    return words[0].rearrange("p c r -> p (c r)").bitcast(I32)
+
+
+def deal(nc, dst, src, run):
+    nc.vector.tensor_copy(
+        dst.rearrange("p (t c i) -> p c t i", t=PACK, i=run),
+        src.rearrange("p (c i t) -> p c t i", t=PACK, i=run),
+    )
+
+
+def place_scale_rows(queues, dst, src):
+    for e in range(4):
+        queues[e % 2].dma_start(dst[e:P:32, :].bitcast(I32), src[8 * e : P : 32, :].bitcast(I32))
+
+
+def tile_picked_pqmixhoppsend_none_po_kernel(
+    tc, x_words, x_scales, d_words, d_scales, gn, w1_words, w1_scales, w2_words, w2_scales,
+    offs, k1, n1, n2, two, n3, out_0, out_1, out_2,
+):
+    nc = tc.nc
+    with ExitStack() as ctx:
+        sb = ctx.enter_context(tc.tile_pool(name="sb", bufs=1))
+        ps = ctx.enter_context(tc.psum_pool(name="ps", bufs=1))
+
+        def tile(name, shape, dtype, tag=None, bufs=1):
+            return sb.tile(shape, dtype, name=name, tag=tag or name, bufs=bufs, align_bytes=64)
+
+        def load_list(name, src):
+            lst = tile(name, list(src.shape), U16)
+            nc.sync.dma_start(lst[:], src)
+            return lst
+
+        d_bytes = tile("d_bytes", [P, G], U8, tag="d_bytes_then_w_raw")
+        x_bytes = tile("x_bytes", [P, T], U8, tag="x_bytes_then_w_placed")
+        placed = tile("placed", [P, H + 2 * S], U8)
+        nc.vector.memset(d_bytes[:, 0 : G // 2].bitcast(I32), 0)
+        nc.gpsimd.memset(d_bytes[:, G // 2 :].bitcast(I32), 0)
+        nc.vector.memset(x_bytes[:].bitcast(I32), 0)
+        nc.gpsimd.memset(placed[:].bitcast(I32), 0)
+        h = [tile("h%d" % t, [P, S + SPARE], F32) for t in range(PACK)]
+        for t in range(PACK):
+            nc.gpsimd.memset(h[t][:, S:], 0.0)
+        k1_l = load_list("k1_l", k1)
+        nc.scalar.dma_start(d_bytes[0:P:8, :].bitcast(I32), d_scales[0].bitcast(I32))
+        offs_l = load_list("offs_l", offs)
+        nc.scalar.dma_start(x_bytes[0:P:8, :].bitcast(I32), x_scales[0].bitcast(I32))
+        x_tab = tile("x_tab", [P, T], U32)
+        nc.sync.dma_start(x_tab[:].bitcast(I32), words_in_dram(x_words))
+        d_tab = tile("d_tab", [P, G], U32)
+        nc.sync.dma_start(d_tab[:].bitcast(I32), words_in_dram(d_words))
+        two_l = load_list("two_l", two)
+        n1_l = load_list("n1_l", n1)
+        n2_l = load_list("n2_l", n2)
+        n3_l = load_list("n3_l", n3)
+        gain = tile("gain", [P, PACK], F32)
+        nc.sync.dma_start(gain[:], gn.rearrange("(p t) o -> p (t o)", t=PACK))
+
+        picked = tile("picked", [P, H + 2 * S], U8)
+        nc.vector.tensor_copy(picked[:, 0:H], d_bytes[:].indirect(k1_l[:]))
+        nc.vector.tensor_copy(picked[:, H : H + S], x_bytes[:].indirect(offs_l[:]))
+        nc.vector.tensor_copy(picked[:, H + S :], x_bytes[:].indirect(two_l[:]))
+        place_scale_rows((nc.scalar, nc.scalar), placed, picked)
+
+        w_raw = tile("w_raw", [P, 2 * N], U32, tag="d_bytes_then_w_raw")
+        nc.sync.dma_start(w_raw[:, N : 2 * N].bitcast(I32), words_in_dram(w2_words))
+        nc.sync.dma_start(w_raw[:, 0:N].bitcast(I32), words_in_dram(w1_words))
+        w_placed = tile("w_placed", [P, N], U8, tag="x_bytes_then_w_placed")
+        nc.gpsimd.memset(w_placed[:].bitcast(I32), 0)
+        for w, scales in enumerate((w1_scales, w2_scales)):
+            for q in range(4):
+                first = 32 * q + 4 * w
+                nc.sync.dma_start(w_placed[first : first + 4, :].bitcast(I32), scales[0, 4 * q : 4 * q + 4, :].bitcast(I32))
+
+        xq = tile("xq", [P, S], U32)
+        nc.vector.tensor_copy(xq[:], x_tab[:].indirect(offs_l[:]))
+        d_picked = tile("d_picked", [P, H], U32)
+        nc.vector.tensor_copy(d_picked[:], d_tab[:].indirect(k1_l[:]))
+        d_codes = tile("d_codes", [P, H], U32)
+        deal(nc, d_codes[:].bitcast(I32), d_picked[:].bitcast(I32), 4)
+        d_scale = tile("d_scale", [P, H], U8)
+        deal(nc, d_scale[:], placed[:, 0:H], 16)
+
+        h_ps = [ps.tile([P, S], F32, name="h_ps%d" % t) for t in range(PACK)]
+        for t in range(PACK):
+            cols = slice(t * P, (t + 1) * P)
+            nc.tensor.matmul_mx(h_ps[t][:], lhsT=d_codes[:, cols].bitcast(FP8X4), lhsT_scale=d_scale[:, cols],
+                                rhs=xq[:].bitcast(FP8X4), rhs_scale=placed[:, H : H + S], start=True, stop=True)
+
+        x_two = tile("x_two", [P, S], U32)
+        nc.vector.tensor_copy(x_two[:], x_tab[:].indirect(two_l[:]))
+
+        st = [tile("st%d" % t, [P, S], F32) for t in range(PACK)]
+        th = [tile("th%d" % t, [P, S], F32) for t in range(PACK)]
+        for t in range(PACK):
+            if t == 0:
+                nc.scalar.activation(h[t][:, 0:S], h_ps[t][:], ACT.Copy, scale=0.0625)
+            else:
+                nc.vector.tensor_scalar(h[t][:, 0:S], h_ps[t][:], 0.0625, None, ALU.mult)
+        for t in range(PACK):
+            hop = tile("hop%d" % t, [P, S], F32, tag="hop", bufs=2)
+            nc.scalar.activation(hop[:], h[t][:].indirect(n1_l[:]), ACT.Copy)
+            nc.vector.scalar_tensor_tensor(st[t][:], h_ps[t][:], 0.0625, hop[:], ALU.mult, ALU.add)
+            nc.scalar.activation(th[t][:], st[t][:], ACT.Tanh)
+
+        w_codes = tile("w_codes", [P, 2 * N], U32)
+        deal(nc, w_codes[:].bitcast(I32), w_raw[:].bitcast(I32), 4)
+        w_scale = tile("w_scale", [P, N], U8)
+        deal(nc, w_scale[:], w_placed[:], 16)
+
+        h2_ps = [ps.tile([P, S], F32, name="h2_ps%d" % t) for t in range(PACK)]
+
+        def w2_pass(t, half):
+            toks = slice(half * HALF, (half + 1) * HALF)
+            nc.tensor.matmul_mx(h2_ps[t][:, toks], lhsT=w_codes[:, (2 * t + 1) * P : (2 * t + 2) * P].bitcast(FP8X4),
+                                lhsT_scale=w_scale[4:P, t * P : (t + 1) * P],
+                                rhs=x_two[:, toks].bitcast(FP8X4),
+                                rhs_scale=placed[:, H + S + half * HALF : H + S + (half + 1) * HALF],
+                                start=True, stop=False)
+
+        for t in range(PACK):
+            w2_pass(t, 0)
+
+        ds = [tile("ds%d" % t, [P, S], F32) for t in range(PACK)]
+        for half in range(2):
+            toks = slice(half * HALF, (half + 1) * HALF)
+            entries = slice(half * HALF // 16, (half + 1) * HALF // 16)
+            z_bf = tile("z_bf%d" % half, [P, HALF, PACK], BF16)
+            for t in range(PACK):
+                prod = tile("prod%d_%d" % (half, t), [P, HALF], F32)
+                nc.vector.tensor_tensor(prod[:], th[t][:].indirect(n2_l[:, entries]), st[t][:, toks], ALU.mult)
+                nc.vector.tensor_scalar(z_bf[:, :, t], prod[:], gain[:, t : t + 1], None, ALU.mult)
+            z_codes = tile("z_codes%d" % half, [P, HALF], U32)
+            z_scale = tile("z_scale%d" % half, [P, HALF], U8)
+            nc.vector.quantize_mx(z_codes[:].bitcast(FP8X4), z_scale[:], z_bf[:].rearrange("p j t -> p (j t)"))
+            for t in range(PACK):
+                if half == 1:
+                    w2_pass(t, half)
+                nc.tensor.matmul_mx(h2_ps[t][:, toks], lhsT=w_codes[:, 2 * t * P : (2 * t + 1) * P].bitcast(FP8X4),
+                                    lhsT_scale=w_scale[:, t * P : (t + 1) * P],
+                                    rhs=z_codes[:].bitcast(FP8X4), rhs_scale=z_scale[:], start=False, stop=True)
+                rl = tile("rl%d_%d" % (half, t), [P, HALF], F32)
+                nc.vector.tensor_scalar(rl[:], h2_ps[t][:, toks], 0.0, None, ALU.max)
+                nc.scalar.activation(ds[t][:].indirect(n3_l[:, entries]), rl[:], ACT.Copy)
+
+        y = tile("y", [P, PACK, S], F32)
+        y_bf = tile("y_bf", [P, S, PACK], BF16)
+        out_rows = out_0.rearrange("(p t) j -> p t j", t=PACK)
+        for t in range(PACK):
+            nc.vector.scalar_tensor_tensor(y[:, t, :], h2_ps[t][:], -0.5, ds[t][:], ALU.mult, ALU.add)
+            nc.sync.dma_start(out_rows[:, t, :], y[:, t, :])
+            if t % 2 == 1:
+                nc.vector.tensor_copy(y_bf[:, :, t - 1 : t + 1], y[:, t - 1 : t + 1, :].rearrange("p t j -> p j t"))
+        y_codes = tile("y_codes", [P, S], U32)
+        y_scale = tile("y_scale", [P, S], U8)
+        nc.vector.quantize_mx(y_codes[:].bitcast(FP8X4), y_scale[:], y_bf[:].rearrange("p j t -> p (j t)"))
+        nc.sync.dma_start(words_in_dram(out_1), y_codes[:].bitcast(I32))
+        for q in range(4):
+            (nc.scalar, nc.sync)[q % 2].dma_start(
+                out_2[0, 4 * q : 4 * q + 4, :].bitcast(I32), y_scale[32 * q : 32 * q + 4, :].bitcast(I32))

@@ -25,16 +25,21 @@ def words_in_dram(words):
     return words[0].rearrange("p c r -> p (c r)").bitcast(I32)
 
 
-def deal(nc, dst, src, run):
-    nc.vector.tensor_copy(
+def rows_times_8(scales):
+    rows = scales[0].bitcast(I32)
+    return rows.unsqueeze(1).to_broadcast([16, 8, rows.shape[1]])
+
+
+def deal(engine, dst, src, run):
+    engine.tensor_copy(
         dst.rearrange("p (t c i) -> p c t i", t=PACK, i=run),
         src.rearrange("p (c i t) -> p c t i", t=PACK, i=run),
     )
 
 
-def place_scale_rows(queues, dst, src):
-    for e in range(4):
-        queues[e % 2].dma_start(dst[e:P:32, :].bitcast(I32), src[8 * e : P : 32, :].bitcast(I32))
+def place_scale_rows(queue, plane):
+    for e in range(1, 4):
+        queue.dma_start(plane[e:P:32, :].bitcast(I32), plane[8 * e : P : 32, :].bitcast(I32))
 
 
 def tile_picked_pqmixhoppsend_none_po_kernel(
@@ -54,63 +59,63 @@ def tile_picked_pqmixhoppsend_none_po_kernel(
             nc.sync.dma_start(lst[:], src)
             return lst
 
-        d_bytes = tile("d_bytes", [P, G], U8, tag="d_bytes_then_w_raw")
-        x_bytes = tile("x_bytes", [P, T], U8, tag="x_bytes_then_w_placed")
-        placed = tile("placed", [P, H + 2 * S], U8)
-        nc.vector.memset(d_bytes[:, 0 : G // 2].bitcast(I32), 0)
-        nc.gpsimd.memset(d_bytes[:, G // 2 :].bitcast(I32), 0)
-        nc.vector.memset(x_bytes[:].bitcast(I32), 0)
-        nc.gpsimd.memset(placed[:].bitcast(I32), 0)
-        h = [tile("h%d" % t, [P, S + SPARE], F32) for t in range(PACK)]
+        d_bytes = tile("d_bytes", [P, G], U8)
+        x_bytes = tile("x_bytes", [P, T], U8, tag="x_bytes_then_gain")
+        w_bytes = [tile("w_bytes%d" % w, [P, N], U8) for w in range(2)]
+        h = [tile("h%d" % t, [P, S + SPARE], F32, tag="h%d" % t) for t in range(PACK)]
         for t in range(PACK):
             nc.gpsimd.memset(h[t][:, S:], 0.0)
         k1_l = load_list("k1_l", k1)
-        nc.scalar.dma_start(d_bytes[0:P:8, :].bitcast(I32), d_scales[0].bitcast(I32))
+        nc.scalar.dma_start(d_bytes[:].bitcast(I32), rows_times_8(d_scales))
         offs_l = load_list("offs_l", offs)
-        nc.scalar.dma_start(x_bytes[0:P:8, :].bitcast(I32), x_scales[0].bitcast(I32))
+        nc.sync.dma_start(x_bytes[:].bitcast(I32), rows_times_8(x_scales))
+        two_l = load_list("two_l", two)
+        nc.sync.dma_start(w_bytes[0][:].bitcast(I32), rows_times_8(w1_scales))
         x_tab = tile("x_tab", [P, T], U32)
         nc.sync.dma_start(x_tab[:].bitcast(I32), words_in_dram(x_words))
         d_tab = tile("d_tab", [P, G], U32)
         nc.sync.dma_start(d_tab[:].bitcast(I32), words_in_dram(d_words))
-        two_l = load_list("two_l", two)
+        nc.sync.dma_start(w_bytes[1][:].bitcast(I32), rows_times_8(w2_scales))
         n1_l = load_list("n1_l", n1)
         n2_l = load_list("n2_l", n2)
         n3_l = load_list("n3_l", n3)
-        gain = tile("gain", [P, PACK], F32)
-        nc.sync.dma_start(gain[:], gn.rearrange("(p t) o -> p (t o)", t=PACK))
 
-        picked = tile("picked", [P, H + 2 * S], U8)
+        picked = tile("picked", [P, H + S], U8, tag="picked_then_w_raw")
+        placed = tile("placed", [P, H + S], U8)
         nc.vector.tensor_copy(picked[:, 0:H], d_bytes[:].indirect(k1_l[:]))
-        nc.vector.tensor_copy(picked[:, H : H + S], x_bytes[:].indirect(offs_l[:]))
-        nc.vector.tensor_copy(picked[:, H + S :], x_bytes[:].indirect(two_l[:]))
-        place_scale_rows((nc.scalar, nc.scalar), placed, picked)
+        nc.vector.tensor_copy(picked[:, H:], x_bytes[:].indirect(offs_l[:]))
+        deal(nc.vector, placed[:, 0:H], picked[:, 0:H], 16)
+        nc.vector.tensor_copy(placed[:, H:].bitcast(I32), picked[:, H:].bitcast(I32))
+        place_scale_rows(nc.sync, placed)
 
-        w_raw = tile("w_raw", [P, 2 * N], U32, tag="d_bytes_then_w_raw")
-        nc.sync.dma_start(w_raw[:, N : 2 * N].bitcast(I32), words_in_dram(w2_words))
-        nc.sync.dma_start(w_raw[:, 0:N].bitcast(I32), words_in_dram(w1_words))
-        w_placed = tile("w_placed", [P, N], U8, tag="x_bytes_then_w_placed")
-        nc.gpsimd.memset(w_placed[:].bitcast(I32), 0)
-        for w, scales in enumerate((w1_scales, w2_scales)):
-            for q in range(4):
-                first = 32 * q + 4 * w
-                nc.sync.dma_start(w_placed[first : first + 4, :].bitcast(I32), scales[0, 4 * q : 4 * q + 4, :].bitcast(I32))
+        w_raw = tile("w_raw", [P, 2, N], U32, tag="picked_then_w_raw")
+        nc.sync.dma_start(w_raw[:, 1, :].bitcast(I32), words_in_dram(w2_words))
+        nc.sync.dma_start(w_raw[:, 0, :].bitcast(I32), words_in_dram(w1_words))
 
         xq = tile("xq", [P, S], U32)
         nc.vector.tensor_copy(xq[:], x_tab[:].indirect(offs_l[:]))
-        d_picked = tile("d_picked", [P, H], U32)
+        d_picked = tile("d_picked", [P, H], U32, tag="d_picked_then_x_two")
         nc.vector.tensor_copy(d_picked[:], d_tab[:].indirect(k1_l[:]))
         d_codes = tile("d_codes", [P, H], U32)
-        deal(nc, d_codes[:].bitcast(I32), d_picked[:].bitcast(I32), 4)
-        d_scale = tile("d_scale", [P, H], U8)
-        deal(nc, d_scale[:], placed[:, 0:H], 16)
+        deal(nc.vector, d_codes[:].bitcast(I32), d_picked[:].bitcast(I32), 4)
+
+        two_picked = tile("two_picked", [P, S], U8)
+        nc.vector.tensor_copy(two_picked[:], x_bytes[:].indirect(two_l[:]))
+        placed2 = tile("placed2", [P, 2 * N + S], U8)
+        for w in range(2):
+            deal(nc.gpsimd, placed2[:, w * N : (w + 1) * N], w_bytes[w][:], 16)
+        nc.vector.tensor_copy(placed2[:, 2 * N :].bitcast(I32), two_picked[:].bitcast(I32))
+        place_scale_rows(nc.sync, placed2)
+        gain = tile("gain", [P, PACK], F32, tag="x_bytes_then_gain")
+        nc.sync.dma_start(gain[:], gn.rearrange("(p t) o -> p (t o)", t=PACK))
 
         h_ps = [ps.tile([P, S], F32, name="h_ps%d" % t) for t in range(PACK)]
         for t in range(PACK):
             cols = slice(t * P, (t + 1) * P)
-            nc.tensor.matmul_mx(h_ps[t][:], lhsT=d_codes[:, cols].bitcast(FP8X4), lhsT_scale=d_scale[:, cols],
-                                rhs=xq[:].bitcast(FP8X4), rhs_scale=placed[:, H : H + S], start=True, stop=True)
+            nc.tensor.matmul_mx(h_ps[t][:], lhsT=d_codes[:, cols].bitcast(FP8X4), lhsT_scale=placed[:, cols],
+                                rhs=xq[:].bitcast(FP8X4), rhs_scale=placed[:, H:], start=True, stop=True)
 
-        x_two = tile("x_two", [P, S], U32)
+        x_two = tile("x_two", [P, S], U32, tag="d_picked_then_x_two")
         nc.vector.tensor_copy(x_two[:], x_tab[:].indirect(two_l[:]))
 
         st = [tile("st%d" % t, [P, S], F32) for t in range(PACK)]
@@ -126,19 +131,18 @@ def tile_picked_pqmixhoppsend_none_po_kernel(
             nc.vector.scalar_tensor_tensor(st[t][:], h_ps[t][:], 0.0625, hop[:], ALU.mult, ALU.add)
             nc.scalar.activation(th[t][:], st[t][:], ACT.Tanh)
 
-        w_codes = tile("w_codes", [P, 2 * N], U32)
-        deal(nc, w_codes[:].bitcast(I32), w_raw[:].bitcast(I32), 4)
-        w_scale = tile("w_scale", [P, N], U8)
-        deal(nc, w_scale[:], w_placed[:], 16)
+        w_codes = [tile("w_codes%d" % w, [P, N], U32) for w in range(2)]
+        for w in (1, 0):
+            deal(nc.gpsimd, w_codes[w][:].bitcast(I32), w_raw[:, w, :].bitcast(I32), 4)
 
         h2_ps = [ps.tile([P, S], F32, name="h2_ps%d" % t) for t in range(PACK)]
 
         def w2_pass(t, half):
             toks = slice(half * HALF, (half + 1) * HALF)
-            nc.tensor.matmul_mx(h2_ps[t][:, toks], lhsT=w_codes[:, (2 * t + 1) * P : (2 * t + 2) * P].bitcast(FP8X4),
-                                lhsT_scale=w_scale[4:P, t * P : (t + 1) * P],
+            nc.tensor.matmul_mx(h2_ps[t][:, toks], lhsT=w_codes[1][:, t * P : (t + 1) * P].bitcast(FP8X4),
+                                lhsT_scale=placed2[:, N + t * P : N + (t + 1) * P],
                                 rhs=x_two[:, toks].bitcast(FP8X4),
-                                rhs_scale=placed[:, H + S + half * HALF : H + S + (half + 1) * HALF],
+                                rhs_scale=placed2[:, 2 * N + half * HALF : 2 * N + (half + 1) * HALF],
                                 start=True, stop=False)
 
         for t in range(PACK):
@@ -148,19 +152,22 @@ def tile_picked_pqmixhoppsend_none_po_kernel(
         for half in range(2):
             toks = slice(half * HALF, (half + 1) * HALF)
             entries = slice(half * HALF // 16, (half + 1) * HALF // 16)
-            z_bf = tile("z_bf%d" % half, [P, HALF, PACK], BF16)
+            prod = tile("prod%d" % half, [P, PACK, HALF], F32, tag=("prod0", "h3")[half])
+            z_bf = tile("z_bf%d" % half, [P, HALF, PACK], BF16, tag=("h3", "z_bf1")[half])
             for t in range(PACK):
-                prod = tile("prod%d_%d" % (half, t), [P, HALF], F32)
-                nc.vector.tensor_tensor(prod[:], th[t][:].indirect(n2_l[:, entries]), st[t][:, toks], ALU.mult)
-                nc.vector.tensor_scalar(z_bf[:, :, t], prod[:], gain[:, t : t + 1], None, ALU.mult)
+                nc.vector.tensor_tensor(prod[:, t, :], th[t][:].indirect(n2_l[:, entries]), st[t][:, toks], ALU.mult)
+                if half == 0 and t < 2:
+                    nc.scalar.activation(z_bf[:, :, t], prod[:, t, :], ACT.Copy, scale=gain[:, t : t + 1])
+                else:
+                    nc.vector.tensor_scalar(z_bf[:, :, t], prod[:, t, :], gain[:, t : t + 1], None, ALU.mult)
             z_codes = tile("z_codes%d" % half, [P, HALF], U32)
             z_scale = tile("z_scale%d" % half, [P, HALF], U8)
             nc.vector.quantize_mx(z_codes[:].bitcast(FP8X4), z_scale[:], z_bf[:].rearrange("p j t -> p (j t)"))
             for t in range(PACK):
                 if half == 1:
                     w2_pass(t, half)
-                nc.tensor.matmul_mx(h2_ps[t][:, toks], lhsT=w_codes[:, 2 * t * P : (2 * t + 1) * P].bitcast(FP8X4),
-                                    lhsT_scale=w_scale[:, t * P : (t + 1) * P],
+                nc.tensor.matmul_mx(h2_ps[t][:, toks], lhsT=w_codes[0][:, t * P : (t + 1) * P].bitcast(FP8X4),
+                                    lhsT_scale=placed2[:, t * P : (t + 1) * P],
                                     rhs=z_codes[:].bitcast(FP8X4), rhs_scale=z_scale[:], start=False, stop=True)
                 rl = tile("rl%d_%d" % (half, t), [P, HALF], F32)
                 nc.vector.tensor_scalar(rl[:], h2_ps[t][:, toks], 0.0, None, ALU.max)
@@ -169,14 +176,18 @@ def tile_picked_pqmixhoppsend_none_po_kernel(
         y = tile("y", [P, PACK, S], F32)
         y_bf = tile("y_bf", [P, S, PACK], BF16)
         out_rows = out_0.rearrange("(p t) j -> p t j", t=PACK)
-        for t in range(PACK):
-            nc.vector.scalar_tensor_tensor(y[:, t, :], h2_ps[t][:], -0.5, ds[t][:], ALU.mult, ALU.add)
-            nc.sync.dma_start(out_rows[:, t, :], y[:, t, :])
-            if t % 2 == 1:
-                nc.vector.tensor_copy(y_bf[:, :, t - 1 : t + 1], y[:, t - 1 : t + 1, :].rearrange("p t j -> p j t"))
         y_codes = tile("y_codes", [P, S], U32)
         y_scale = tile("y_scale", [P, S], U8)
-        nc.vector.quantize_mx(y_codes[:].bitcast(FP8X4), y_scale[:], y_bf[:].rearrange("p j t -> p (j t)"))
+        halves = [slice(0, HALF), slice(HALF, S)]
+        for t in range(PACK):
+            for toks in halves if t == PACK - 1 else [slice(0, S)]:
+                nc.vector.scalar_tensor_tensor(y[:, t, toks], h2_ps[t][:, toks], -0.5, ds[t][:, toks], ALU.mult, ALU.add)
+            nc.sync.dma_start(out_rows[:, t, :], y[:, t, :])
+            if t % 2 == 1:
+                for toks in halves if t == PACK - 1 else [slice(0, S)]:
+                    nc.vector.tensor_copy(y_bf[:, toks, t - 1 : t + 1], y[:, t - 1 : t + 1, toks].rearrange("p t j -> p j t"))
+        for toks in halves:
+            nc.vector.quantize_mx(y_codes[:, toks].bitcast(FP8X4), y_scale[:, toks], y_bf[:, toks, :].rearrange("p j t -> p (j t)"))
         nc.sync.dma_start(words_in_dram(out_1), y_codes[:].bitcast(I32))
         for q in range(4):
             (nc.scalar, nc.sync)[q % 2].dma_start(

@@ -37,9 +37,9 @@ def deal(engine, dst, src, run):
     )
 
 
-def place_scale_rows(queue, plane):
+def place_scale_rows(queue, plane, first):
     for e in range(1, 4):
-        queue.dma_start(plane[e:P:32, :].bitcast(I32), plane[8 * e : P : 32, :].bitcast(I32))
+        queue.dma_start(plane[first + e : P : 32, :].bitcast(I32), plane[first + 8 * e : P : 32, :].bitcast(I32))
 
 
 def tile_picked_pqmixhoppsend_none_po_kernel(
@@ -60,54 +60,59 @@ def tile_picked_pqmixhoppsend_none_po_kernel(
             return lst
 
         d_bytes = tile("d_bytes", [P, G], U8)
-        x_bytes = tile("x_bytes", [P, T], U8, tag="x_bytes_then_gain")
-        w_bytes = [tile("w_bytes%d" % w, [P, N], U8) for w in range(2)]
+        x_bytes = tile("x_bytes", [P, T], U8)
+        w_bytes = tile("w_bytes", [P, N], U8)
+        nc.gpsimd.memset(w_bytes[:].bitcast(I32), 0)
         h = [tile("h%d" % t, [P, S + SPARE], F32, tag="h%d" % t) for t in range(PACK)]
         for t in range(PACK):
             nc.gpsimd.memset(h[t][:, S:], 0.0)
+        gain = tile("gain", [P, PACK], F32)
+        nc.gpsimd.dma_start(gain[:], gn.rearrange("(p t) o -> p (t o)", t=PACK))
         k1_l = load_list("k1_l", k1)
         nc.scalar.dma_start(d_bytes[:].bitcast(I32), rows_times_8(d_scales))
         offs_l = load_list("offs_l", offs)
         nc.sync.dma_start(x_bytes[:].bitcast(I32), rows_times_8(x_scales))
+        d_tab = tile("d_tab", [P, G], U32, tag="d_tab_then_xq")
+        nc.sync.dma_start(d_tab[:].bitcast(I32), words_in_dram(d_words))
         two_l = load_list("two_l", two)
-        nc.sync.dma_start(w_bytes[0][:].bitcast(I32), rows_times_8(w1_scales))
+        n1_l = load_list("n1_l", n1)
         x_tab = tile("x_tab", [P, T], U32)
         nc.sync.dma_start(x_tab[:].bitcast(I32), words_in_dram(x_words))
-        d_tab = tile("d_tab", [P, G], U32)
-        nc.sync.dma_start(d_tab[:].bitcast(I32), words_in_dram(d_words))
-        nc.sync.dma_start(w_bytes[1][:].bitcast(I32), rows_times_8(w2_scales))
-        n1_l = load_list("n1_l", n1)
         n2_l = load_list("n2_l", n2)
         n3_l = load_list("n3_l", n3)
+        nc.sync.dma_start(w_bytes[0:P:8, :].bitcast(I32), w1_scales[0].bitcast(I32))
+        nc.sync.dma_start(w_bytes[4:P:8, :].bitcast(I32), w2_scales[0].bitcast(I32))
 
-        picked = tile("picked", [P, H + S], U8, tag="picked_then_w_raw")
+        d_bytes_picked = tile("d_bytes_picked", [P, H], U8)
+        x_bytes_picked = tile("x_bytes_picked", [P, S], U8, tag="x_bytes_picked_then_w_raw")
         placed = tile("placed", [P, H + S], U8)
-        nc.vector.tensor_copy(picked[:, 0:H], d_bytes[:].indirect(k1_l[:]))
-        nc.vector.tensor_copy(picked[:, H:], x_bytes[:].indirect(offs_l[:]))
-        deal(nc.vector, placed[:, 0:H], picked[:, 0:H], 16)
-        nc.vector.tensor_copy(placed[:, H:].bitcast(I32), picked[:, H:].bitcast(I32))
-        place_scale_rows(nc.sync, placed)
+        nc.vector.tensor_copy(d_bytes_picked[:], d_bytes[:].indirect(k1_l[:]))
+        nc.vector.tensor_copy(x_bytes_picked[:], x_bytes[:].indirect(offs_l[:]))
+        deal(nc.vector, placed[:, 0:H], d_bytes_picked[:], 16)
+        nc.vector.tensor_copy(placed[:, H:].bitcast(I32), x_bytes_picked[:].bitcast(I32))
+        place_scale_rows(nc.sync, placed[:], 0)
 
-        w_raw = tile("w_raw", [P, 2, N], U32, tag="picked_then_w_raw")
+        w_raw = tile("w_raw", [P, 2, N], U32, tag="x_bytes_picked_then_w_raw")
         nc.sync.dma_start(w_raw[:, 1, :].bitcast(I32), words_in_dram(w2_words))
         nc.sync.dma_start(w_raw[:, 0, :].bitcast(I32), words_in_dram(w1_words))
 
-        xq = tile("xq", [P, S], U32)
+        d_picked = [tile("d_picked%d" % u, [P, H // 2], U32, tag="d_picked%d" % u) for u in range(2)]
+        for u in range(2):
+            nc.vector.tensor_copy(d_picked[u][:], d_tab[:].indirect(k1_l[:, u * 16 : (u + 1) * 16]))
+        xq = tile("xq", [P, S], U32, tag="d_tab_then_xq")
         nc.vector.tensor_copy(xq[:], x_tab[:].indirect(offs_l[:]))
-        d_picked = tile("d_picked", [P, H], U32, tag="d_picked_then_x_two")
-        nc.vector.tensor_copy(d_picked[:], d_tab[:].indirect(k1_l[:]))
         d_codes = tile("d_codes", [P, H], U32)
-        deal(nc.vector, d_codes[:].bitcast(I32), d_picked[:].bitcast(I32), 4)
+        d_dealt = d_codes[:].bitcast(I32).rearrange("p (t u c i) -> p u c t i", t=PACK, u=2, i=4)
+        for u in range(2):
+            nc.vector.tensor_copy(d_dealt[:, u], d_picked[u][:].bitcast(I32).rearrange("p (c i t) -> p c t i", t=PACK, i=4))
 
-        two_picked = tile("two_picked", [P, S], U8)
+        placed2 = tile("placed2", [P, N + S], U8, tag="d_picked0")
+        deal(nc.vector, placed2[:, 0:N], w_bytes[:], 16)
+        place_scale_rows(nc.sync, placed2[:, 0:N], 4)
+        two_picked = tile("two_picked", [P, S], U8, tag="d_picked1")
         nc.vector.tensor_copy(two_picked[:], x_bytes[:].indirect(two_l[:]))
-        placed2 = tile("placed2", [P, 2 * N + S], U8)
-        for w in range(2):
-            deal(nc.gpsimd, placed2[:, w * N : (w + 1) * N], w_bytes[w][:], 16)
-        nc.vector.tensor_copy(placed2[:, 2 * N :].bitcast(I32), two_picked[:].bitcast(I32))
-        place_scale_rows(nc.sync, placed2)
-        gain = tile("gain", [P, PACK], F32, tag="x_bytes_then_gain")
-        nc.sync.dma_start(gain[:], gn.rearrange("(p t) o -> p (t o)", t=PACK))
+        nc.vector.tensor_copy(placed2[:, N:].bitcast(I32), two_picked[:].bitcast(I32))
+        place_scale_rows(nc.sync, placed2[:], 0)
 
         h_ps = [ps.tile([P, S], F32, name="h_ps%d" % t) for t in range(PACK)]
         for t in range(PACK):
@@ -115,13 +120,13 @@ def tile_picked_pqmixhoppsend_none_po_kernel(
             nc.tensor.matmul_mx(h_ps[t][:], lhsT=d_codes[:, cols].bitcast(FP8X4), lhsT_scale=placed[:, cols],
                                 rhs=xq[:].bitcast(FP8X4), rhs_scale=placed[:, H:], start=True, stop=True)
 
-        x_two = tile("x_two", [P, S], U32, tag="d_picked_then_x_two")
+        x_two = tile("x_two", [P, S], U32, tag="d_picked1")
         nc.vector.tensor_copy(x_two[:], x_tab[:].indirect(two_l[:]))
 
         st = [tile("st%d" % t, [P, S], F32) for t in range(PACK)]
         th = [tile("th%d" % t, [P, S], F32) for t in range(PACK)]
         for t in range(PACK):
-            if t == 0:
+            if t < 2:
                 nc.scalar.activation(h[t][:, 0:S], h_ps[t][:], ACT.Copy, scale=0.0625)
             else:
                 nc.vector.tensor_scalar(h[t][:, 0:S], h_ps[t][:], 0.0625, None, ALU.mult)
@@ -131,18 +136,18 @@ def tile_picked_pqmixhoppsend_none_po_kernel(
             nc.vector.scalar_tensor_tensor(st[t][:], h_ps[t][:], 0.0625, hop[:], ALU.mult, ALU.add)
             nc.scalar.activation(th[t][:], st[t][:], ACT.Tanh)
 
-        w_codes = [tile("w_codes%d" % w, [P, N], U32) for w in range(2)]
+        w_codes = [tile("w_codes%d" % w, [P, N], U32, tag="h%d" % (1 - w)) for w in range(2)]
         for w in (1, 0):
-            deal(nc.gpsimd, w_codes[w][:].bitcast(I32), w_raw[:, w, :].bitcast(I32), 4)
+            deal(nc.vector, w_codes[w][:].bitcast(I32), w_raw[:, w, :].bitcast(I32), 4)
 
         h2_ps = [ps.tile([P, S], F32, name="h2_ps%d" % t) for t in range(PACK)]
 
         def w2_pass(t, half):
             toks = slice(half * HALF, (half + 1) * HALF)
             nc.tensor.matmul_mx(h2_ps[t][:, toks], lhsT=w_codes[1][:, t * P : (t + 1) * P].bitcast(FP8X4),
-                                lhsT_scale=placed2[:, N + t * P : N + (t + 1) * P],
+                                lhsT_scale=placed2[4:P, t * P : (t + 1) * P],
                                 rhs=x_two[:, toks].bitcast(FP8X4),
-                                rhs_scale=placed2[:, 2 * N + half * HALF : 2 * N + (half + 1) * HALF],
+                                rhs_scale=placed2[:, N + half * HALF : N + (half + 1) * HALF],
                                 start=True, stop=False)
 
         for t in range(PACK):
@@ -156,7 +161,7 @@ def tile_picked_pqmixhoppsend_none_po_kernel(
             z_bf = tile("z_bf%d" % half, [P, HALF, PACK], BF16, tag=("h3", "z_bf1")[half])
             for t in range(PACK):
                 nc.vector.tensor_tensor(prod[:, t, :], th[t][:].indirect(n2_l[:, entries]), st[t][:, toks], ALU.mult)
-                if half == 0 and t < 2:
+                if half == 0 and t >= 2:
                     nc.scalar.activation(z_bf[:, :, t], prod[:, t, :], ACT.Copy, scale=gain[:, t : t + 1])
                 else:
                     nc.vector.tensor_scalar(z_bf[:, :, t], prod[:, t, :], gain[:, t : t + 1], None, ALU.mult)

from contextlib import ExitStack

import concourse.mybir as mybir

K, T, S, N, G, H = 512, 1024, 256, 512, 2048, 512
FLOPS = 2 * K * H * S + 2 * H * N * S + 2 * K * N * S

F32 = mybir.dt.float32
BF16 = mybir.dt.bfloat16
I32 = mybir.dt.int32
U32 = mybir.dt.uint32
U16 = mybir.dt.uint16
U8 = mybir.dt.uint8
FP8X4 = mybir.dt.float8_e4m3fn_x4
ALU = mybir.AluOpType
ACT = mybir.ActivationFunctionType

P = 128
PACK = 4
HALF = S // 2
SPARE = 16


def words_in_dram(words):
    return words[0].rearrange("p c r -> p (c r)").bitcast(I32)


def rows_times_8(scales):
    rows = scales[0].bitcast(I32)
    return rows.unsqueeze(1).to_broadcast([16, 8, rows.shape[1]])


def deal(engine, dst, src, run):
    engine.tensor_copy(
        dst.rearrange("p (t c i) -> p c t i", t=PACK, i=run),
        src.rearrange("p (c i t) -> p c t i", t=PACK, i=run),
    )


def place_scale_rows(queue, plane, first):
    for e in range(1, 4):
        queue.dma_start(plane[first + e : P : 32, :].bitcast(I32), plane[first + 8 * e : P : 32, :].bitcast(I32))


def tile_picked_pqmixhoppsend_none_po_kernel(
    tc, x_words, x_scales, d_words, d_scales, gn, w1_words, w1_scales, w2_words, w2_scales,
    offs, k1, n1, n2, two, n3, out_0, out_1, out_2,
):
    nc = tc.nc
    with ExitStack() as ctx:
        sb = ctx.enter_context(tc.tile_pool(name="sb", bufs=1))
        ps = ctx.enter_context(tc.psum_pool(name="ps", bufs=1))

        def tile(name, shape, dtype, tag=None, bufs=1):
            return sb.tile(shape, dtype, name=name, tag=tag or name, bufs=bufs, align_bytes=64)

        def load_list(name, src):
            lst = tile(name, list(src.shape), U16)
            nc.sync.dma_start(lst[:], src)
            return lst

        d_bytes = tile("d_bytes", [P, G], U8)
        x_bytes = tile("x_bytes", [P, T], U8)
        w_bytes = tile("w_bytes", [P, N], U8)
        nc.gpsimd.memset(w_bytes[:].bitcast(I32), 0)
        h = [tile("h%d" % t, [P, S + SPARE], F32, tag="h%d" % t) for t in range(PACK)]
        for t in range(PACK):
            nc.gpsimd.memset(h[t][:, S:], 0.0)
        gain = tile("gain", [P, PACK], F32)
        nc.gpsimd.dma_start(gain[:], gn.rearrange("(p t) o -> p (t o)", t=PACK))
        k1_l = load_list("k1_l", k1)
        nc.scalar.dma_start(d_bytes[:].bitcast(I32), rows_times_8(d_scales))
        offs_l = load_list("offs_l", offs)
        nc.sync.dma_start(x_bytes[:].bitcast(I32), rows_times_8(x_scales))
        d_tab = tile("d_tab", [P, G], U32, tag="d_tab_then_xq")
        nc.sync.dma_start(d_tab[:].bitcast(I32), words_in_dram(d_words))
        two_l = load_list("two_l", two)
        n1_l = load_list("n1_l", n1)
        x_tab = tile("x_tab", [P, T], U32)
        nc.sync.dma_start(x_tab[:].bitcast(I32), words_in_dram(x_words))
        n2_l = load_list("n2_l", n2)
        n3_l = load_list("n3_l", n3)
        nc.sync.dma_start(w_bytes[0:P:8, :].bitcast(I32), w1_scales[0].bitcast(I32))
        nc.sync.dma_start(w_bytes[4:P:8, :].bitcast(I32), w2_scales[0].bitcast(I32))

        d_bytes_picked = tile("d_bytes_picked", [P, H], U8)
        x_bytes_picked = tile("x_bytes_picked", [P, S], U8, tag="x_bytes_picked_then_w_raw")
        placed = tile("placed", [P, H + S], U8)
        nc.vector.tensor_copy(d_bytes_picked[:], d_bytes[:].indirect(k1_l[:]))
        nc.vector.tensor_copy(x_bytes_picked[:], x_bytes[:].indirect(offs_l[:]))
        deal(nc.vector, placed[:, 0:H], d_bytes_picked[:], 16)
        nc.vector.tensor_copy(placed[:, H:].bitcast(I32), x_bytes_picked[:].bitcast(I32))
        place_scale_rows(nc.sync, placed[:], 0)

        w_raw = tile("w_raw", [P, 2, N], U32, tag="x_bytes_picked_then_w_raw")
        nc.sync.dma_start(w_raw[:, 1, :].bitcast(I32), words_in_dram(w2_words))
        nc.sync.dma_start(w_raw[:, 0, :].bitcast(I32), words_in_dram(w1_words))

        d_picked = [tile("d_picked%d" % u, [P, H // 2], U32, tag="d_picked%d" % u) for u in range(2)]
        for u in range(2):
            nc.vector.tensor_copy(d_picked[u][:], d_tab[:].indirect(k1_l[:, u * 16 : (u + 1) * 16]))
        xq = tile("xq", [P, S], U32, tag="d_tab_then_xq")
        nc.vector.tensor_copy(xq[:], x_tab[:].indirect(offs_l[:]))
        d_codes = tile("d_codes", [P, H], U32)
        d_dealt = d_codes[:].bitcast(I32).rearrange("p (t u c i) -> p u c t i", t=PACK, u=2, i=4)
        for u in range(2):
            nc.vector.tensor_copy(d_dealt[:, u], d_picked[u][:].bitcast(I32).rearrange("p (c i t) -> p c t i", t=PACK, i=4))

        placed2 = tile("placed2", [P, N + S], U8, tag="d_picked0")
        deal(nc.vector, placed2[:, 0:N], w_bytes[:], 16)
        place_scale_rows(nc.sync, placed2[:, 0:N], 4)
        two_picked = tile("two_picked", [P, S], U8, tag="d_picked1")
        nc.vector.tensor_copy(two_picked[:], x_bytes[:].indirect(two_l[:]))
        nc.vector.tensor_copy(placed2[:, N:].bitcast(I32), two_picked[:].bitcast(I32))
        place_scale_rows(nc.sync, placed2[:], 0)

        h_ps = [ps.tile([P, S], F32, name="h_ps%d" % t) for t in range(PACK)]
        for t in range(PACK):
            cols = slice(t * P, (t + 1) * P)
            nc.tensor.matmul_mx(h_ps[t][:], lhsT=d_codes[:, cols].bitcast(FP8X4), lhsT_scale=placed[:, cols],
                                rhs=xq[:].bitcast(FP8X4), rhs_scale=placed[:, H:], start=True, stop=True)

        x_two = tile("x_two", [P, S], U32, tag="d_picked1")
        nc.vector.tensor_copy(x_two[:], x_tab[:].indirect(two_l[:]))

        st = [tile("st%d" % t, [P, S], F32) for t in range(PACK)]
        th = [tile("th%d" % t, [P, S], F32) for t in range(PACK)]
        for t in range(PACK):
            if t < 2:
                nc.scalar.activation(h[t][:, 0:S], h_ps[t][:], ACT.Copy, scale=0.0625)
            else:
                nc.vector.tensor_scalar(h[t][:, 0:S], h_ps[t][:], 0.0625, None, ALU.mult)
        for t in range(PACK):
            hop = tile("hop%d" % t, [P, S], F32, tag="hop", bufs=2)
            nc.scalar.activation(hop[:], h[t][:].indirect(n1_l[:]), ACT.Copy)
            nc.vector.scalar_tensor_tensor(st[t][:], h_ps[t][:], 0.0625, hop[:], ALU.mult, ALU.add)
            nc.scalar.activation(th[t][:], st[t][:], ACT.Tanh)

        w_codes = [tile("w_codes%d" % w, [P, N], U32, tag="h%d" % (1 - w)) for w in range(2)]
        for w in (1, 0):
            deal(nc.vector, w_codes[w][:].bitcast(I32), w_raw[:, w, :].bitcast(I32), 4)

        h2_ps = [ps.tile([P, S], F32, name="h2_ps%d" % t) for t in range(PACK)]

        def w2_pass(t, half):
            toks = slice(half * HALF, (half + 1) * HALF)
            nc.tensor.matmul_mx(h2_ps[t][:, toks], lhsT=w_codes[1][:, t * P : (t + 1) * P].bitcast(FP8X4),
                                lhsT_scale=placed2[4:P, t * P : (t + 1) * P],
                                rhs=x_two[:, toks].bitcast(FP8X4),
                                rhs_scale=placed2[:, N + half * HALF : N + (half + 1) * HALF],
                                start=True, stop=False)

        for t in range(PACK):
            w2_pass(t, 0)

        ds = [tile("ds%d" % t, [P, S], F32) for t in range(PACK)]
        for half in range(2):
            toks = slice(half * HALF, (half + 1) * HALF)
            entries = slice(half * HALF // 16, (half + 1) * HALF // 16)
            prod = tile("prod%d" % half, [P, PACK, HALF], F32, tag=("prod0", "h3")[half])
            z_bf = tile("z_bf%d" % half, [P, HALF, PACK], BF16, tag=("h3", "z_bf1")[half])
            for t in range(PACK):
                nc.vector.tensor_tensor(prod[:, t, :], th[t][:].indirect(n2_l[:, entries]), st[t][:, toks], ALU.mult)
                if half == 0 and t >= 2:
                    nc.scalar.activation(z_bf[:, :, t], prod[:, t, :], ACT.Copy, scale=gain[:, t : t + 1])
                else:
                    nc.vector.tensor_scalar(z_bf[:, :, t], prod[:, t, :], gain[:, t : t + 1], None, ALU.mult)
            z_codes = tile("z_codes%d" % half, [P, HALF], U32)
            z_scale = tile("z_scale%d" % half, [P, HALF], U8)
            nc.vector.quantize_mx(z_codes[:].bitcast(FP8X4), z_scale[:], z_bf[:].rearrange("p j t -> p (j t)"))
            for t in range(PACK):
                if half == 1:
                    w2_pass(t, half)
                nc.tensor.matmul_mx(h2_ps[t][:, toks], lhsT=w_codes[0][:, t * P : (t + 1) * P].bitcast(FP8X4),
                                    lhsT_scale=placed2[:, t * P : (t + 1) * P],
                                    rhs=z_codes[:].bitcast(FP8X4), rhs_scale=z_scale[:], start=False, stop=True)
                rl = tile("rl%d_%d" % (half, t), [P, HALF], F32)
                nc.vector.tensor_scalar(rl[:], h2_ps[t][:, toks], 0.0, None, ALU.max)
                nc.scalar.activation(ds[t][:].indirect(n3_l[:, entries]), rl[:], ACT.Copy)

        y = tile("y", [P, PACK, S], F32)
        y_bf = tile("y_bf", [P, S, PACK], BF16)
        out_rows = out_0.rearrange("(p t) j -> p t j", t=PACK)
        y_codes = tile("y_codes", [P, S], U32)
        y_scale = tile("y_scale", [P, S], U8)
        halves = [slice(0, HALF), slice(HALF, S)]
        for t in range(PACK):
            for toks in halves if t == PACK - 1 else [slice(0, S)]:
                nc.vector.scalar_tensor_tensor(y[:, t, toks], h2_ps[t][:, toks], -0.5, ds[t][:, toks], ALU.mult, ALU.add)
            nc.sync.dma_start(out_rows[:, t, :], y[:, t, :])
            if t % 2 == 1:
                for toks in halves if t == PACK - 1 else [slice(0, S)]:
                    nc.vector.tensor_copy(y_bf[:, toks, t - 1 : t + 1], y[:, t - 1 : t + 1, toks].rearrange("p t j -> p j t"))
        for toks in halves:
            nc.vector.quantize_mx(y_codes[:, toks].bitcast(FP8X4), y_scale[:, toks], y_bf[:, toks, :].rearrange("p j t -> p (j t)"))
        nc.sync.dma_start(words_in_dram(out_1), y_codes[:].bitcast(I32))
        for q in range(4):
            (nc.scalar, nc.sync)[q % 2].dma_start(
                out_2[0, 4 * q : 4 * q + 4, :].bitcast(I32), y_scale[32 * q : 32 * q + 4, :].bitcast(I32))
